import numpy as np
import ml_dtypes


def mxq(x, axis, fmt="e4m3"):
    dtype, down = {"e4m3": (ml_dtypes.float8_e4m3fn, 7), "e5m2": (ml_dtypes.float8_e5m2, 14)}[fmt]
    v = np.moveaxis(np.asarray(x, np.float32).astype(ml_dtypes.bfloat16).astype(np.float64), axis, -1)
    blocks = v.reshape(v.shape[:-1] + (-1, 32))
    amax = np.abs(blocks).max(-1, keepdims=True)
    byte = np.maximum(np.where(amax > 0, np.frexp(amax)[1] - 1 + 127, 0) - down, 1)
    scale = np.exp2(byte - 127.0)
    codes = (blocks / scale).astype(np.float32).astype(dtype).astype(np.float64)
    return np.moveaxis((codes * scale).reshape(v.shape), -1, axis)


WIDE = False


def mx_kscale(k):
    if not WIDE:
        return np.ones(k)
    levels = np.array([10, -10, 5, -5, 0])
    if k % 512:
        return np.exp2(np.random.permutation(np.resize(levels, k // 32))).repeat(32)
    a = np.empty((k // 512, 16))
    for p in range(k // 512):
        a[p, :8] = np.random.permutation(np.resize(levels, 8))
        for g in range(8):
            far = levels[np.abs(levels - a[p, g]) >= 10]
            a[p, g + 8] = far[np.random.randint(len(far))]
    return np.exp2(a.ravel()).repeat(32)


def f64(x):
    return np.asarray(x).astype(np.float64)


def striped(idx):
    return np.tile(np.asarray(idx).reshape(-1, 16).T, (8, 1)).astype(np.uint16)


def unstriped(offs):
    return offs[:16].T.reshape(-1).astype(np.int64)


def striped8(idx):
    return np.asarray(idx).reshape(8, -1, 16).transpose(0, 2, 1).reshape(128, -1).astype(np.uint16)


def unstriped8(offs):
    return offs.reshape(8, 16, -1).transpose(0, 2, 1).reshape(8, -1).astype(np.int64)


def pick8(x, idx, run):
    r = np.arange(len(x))
    return x[r[:, None], idx[r % (8 * run) // run]]


E2M1 = np.array([0.0, 0.5, 1.0, 1.5, 2.0, 3.0, 4.0, 6.0, -0.0, -0.5, -1.0, -1.5, -2.0, -3.0, -4.0, -6.0])


def pack_weight(w, fmt):
    k, n = w.shape
    w = f64(np.asarray(w, np.float32).astype(ml_dtypes.bfloat16)).reshape(k // 32, 32, n)
    amax = np.abs(w).max(1)
    if fmt == "e4m3":
        byte = np.frexp(amax)[1] - 1 + 127 - 7
    else:
        mant, ex = np.frexp(amax / 6.0)
        byte = np.where(mant > 0.5, ex, ex - 1) + 127
    byte = np.clip(np.where(amax > 0, byte, 1), 1, 254)
    scaled = (w * np.exp2(127.0 - byte)[:, None, :]).reshape(k, n).astype(np.float32)
    by_word = np.ascontiguousarray(scaled.reshape(k // 512, 128, 4, n).transpose(0, 1, 3, 2))
    if fmt == "e4m3":
        words = by_word.astype(ml_dtypes.float8_e4m3fn).view(np.uint8)
    else:
        c = by_word.astype(ml_dtypes.float4_e2m1fn).view(np.uint8) & 0xF
        words = (c[..., 0::2] | (c[..., 1::2] << 4)).reshape(k // 512, 128, 2 * n)
    return np.ascontiguousarray(words), np.ascontiguousarray(byte.astype(np.uint8).reshape(k // 512, 16, n))


def unpack_weight(words, scales, fmt):
    g, _, n = scales.shape
    words = np.ascontiguousarray(words).reshape(g, 128, n, -1)
    if fmt == "e4m3":
        vals = words.view(ml_dtypes.float8_e4m3fn).astype(np.float64)
    else:
        nib = np.empty((g, 128, n, 4), np.uint8)
        nib[..., 0::2] = words & 0xF
        nib[..., 1::2] = words >> 4
        vals = E2M1[nib]
    vals = vals * np.repeat(np.exp2(scales.astype(np.float64) - 127.0), 8, axis=1)[..., None]
    return vals.transpose(0, 1, 3, 2).reshape(g * 512, n)


def sigmoid(v):
    return 1.0 / (1.0 + np.exp(-v))


K, R, F, T, J, U, M = 512, 128, 512, 2048, 512, 1024, 256


def setup_inputs():
    n = np.random.standard_normal
    idx = np.random.permutation(T)[:J]
    idx2 = np.stack([np.random.permutation(U)[:J] for _ in range(8)])
    idx3 = np.stack([np.random.permutation(U)[:M] for _ in range(8)])
    fk = mx_kscale(K)
    ff = mx_kscale(F)
    tabp = pack_weight(n((K, T)) / fk[:, None], "e4m3")
    return {
        "tab_words": tabp[0],
        "tab_scales": tabp[1],
        "w1": (n((K, R)) * 1 / np.sqrt(K) * fk[:, None]).astype(np.float32),
        "gain": (np.random.uniform(0.5, 1.5, (R, 1))).astype(np.float32),
        "pb": (np.random.uniform(0.3, 1.0, (1, M))).astype(np.float32),
        "wo": (n((F, R)) * 1 / np.sqrt(F) * ff[:, None]).astype(np.float32),
        "dy": (n((F, M)) / ff[:, None]).astype(np.float32),
        "old": (0.5 * n((R, J))).astype(np.float32),
        "offs": striped(idx),
        "offs2": striped8(idx2),
        "offs3": striped8(idx3),
    }


def reference(tab_words, tab_scales, w1, gain, pb, wo, dy, old, offs, offs2, offs3):
    idx = unstriped(offs)
    idx2 = unstriped8(offs2)
    idx3 = unstriped8(offs3)
    tabu = unpack_weight(tab_words, tab_scales, "e4m3")
    w1q = mxq(f64(w1), 0, "e4m3")
    tabidxg = tabu[:, idx]
    a = w1q.T @ tabidxg
    h1 = np.tanh(a)
    h2 = h1 * f64(gain)
    pg = np.zeros((R, U))
    pg[np.arange(R)[:, None], idx2[np.arange(R) % 128 // 16]] = h2
    s = pick8(pg, idx3, 16) + f64(pb)
    woq = mxq(f64(wo), 0, "e4m3")
    dyq = mxq(f64(dy), 0, "e4m3")
    c0 = woq.T @ dyq
    ds = c0 * sigmoid(s) + c0 * s * sigmoid(s) * (1.0 - sigmoid(s))
    s1 = np.zeros((R, U))
    s1[np.arange(R)[:, None], idx3[np.arange(R) % 128 // 16]] = ds
    dh2 = pick8(s1, idx2, 16)
    dh1 = dh2 * f64(gain)
    da = dh1 * (1.0 - np.square(h1))
    y = da + f64(old)
    return y

@@ -1,0 +1,176 @@
+from contextlib import ExitStack
+
+import concourse.mybir as mybir
+
+K, R, F, T, J, U, M = 512, 128, 512, 2048, 512, 1024, 256
+FLOPS = 2 * K * R * J + 2 * F * R * M
+
+F32 = mybir.dt.float32
+BF16 = mybir.dt.bfloat16
+I32 = mybir.dt.int32
+U32 = mybir.dt.uint32
+U16 = mybir.dt.uint16
+U8 = mybir.dt.uint8
+FP8X4 = mybir.dt.float8_e4m3fn_x4
+ACT = mybir.ActivationFunctionType
+ALU = mybir.AluOpType
+
+P = 128
+PACK = 4
+GROUP = 16
+HALF = J // 2
+SLOT_PIECES = ((0, 128), (128, 256), (256, 512))
+PICK_PIECES = ((0, 128), (128, 256))
+OUT_PIECES = ((0, 256), (256, 512))
+
+
+def entries(offsets, lo, hi):
+    return offsets[:, lo // GROUP : hi // GROUP]
+
+
+def tile_attend_cwriteread_kernel(tc, tab_words, tab_scales, w1, gain, pb, wo, dy, old, offs, offs2, offs3, out):
+    nc = tc.nc
+    with ExitStack() as ctx:
+        sb = ctx.enter_context(tc.tile_pool(name="sb", bufs=1))
+        ps = ctx.enter_context(tc.psum_pool(name="ps", bufs=1))
+
+        idx = sb.tile([P, J // GROUP], U16, name="idx")
+        idx2 = sb.tile([P, J // GROUP], U16, name="idx2")
+        idx3 = sb.tile([P, M // GROUP], U16, name="idx3")
+        words = sb.tile([P, T], I32, name="words", tag="slot_d", align_bytes=64)
+        scales = sb.tile([P, T], U8, name="scales", tag="slot_c", align_bytes=64)
+        w1_raw = sb.tile([P, PACK, R], F32, name="w1_raw", tag="slot_a", align_bytes=64)
+        gain_col = sb.tile([P, 1], F32, name="gain_col")
+        pg = sb.tile([P, U], F32, name="pg")
+        s1 = sb.tile([P, U], F32, name="s1")
+
+        nc.vector.memset(scales[:].bitcast(I32), 0)
+        nc.sync.dma_start(idx[:], offs)
+        nc.scalar.dma_start(w1_raw[:], w1.rearrange("(p j) r -> p j r", j=PACK))
+        nc.scalar.dma_start(words[:], tab_words[0].rearrange("p n t -> p (n t)").bitcast(I32))
+        for q in range(4):
+            nc.sync.dma_start(
+                scales[32 * q : 32 * q + 4, :].bitcast(I32),
+                tab_scales[0, 4 * q : 4 * q + 4, :].bitcast(I32),
+            )
+        nc.gpsimd.dma_start(gain_col[:], gain)
+        nc.sync.dma_start(idx2[:], offs2)
+        nc.sync.dma_start(idx3[:], offs3)
+        nc.vector.memset(pg[:], 0.0)
+        nc.vector.memset(s1[:], 0.0)
+
+        def interleave(copy, raw, width, name, tag):
+            grouped = sb.tile([P, width, PACK], BF16, name=name, tag=tag, align_bytes=64)
+            copy(grouped[:], raw[:].rearrange("p j w -> p w j"))
+            return grouped
+
+        def quantise(grouped, width, name, codes):
+            plane = sb.tile([P, width], U8, name=name + "_plane", align_bytes=64)
+            nc.vector.quantize_mx(
+                out=codes.bitcast(FP8X4),
+                scales=plane[:],
+                in_=grouped[:].rearrange("p w j -> p (w j)"),
+            )
+            return plane
+
+        gain_rows = sb.tile([P, HALF], F32, name="gain_rows")
+        nc.gpsimd.tensor_scalar(gain_rows[:], gain_col[:].to_broadcast([P, HALF]), 1.0, 0.0, ALU.mult, ALU.add)
+        minus_gain = sb.tile([P, 1], F32, name="minus_gain")
+        nc.gpsimd.tensor_scalar(minus_gain[:], gain_col[:], -1.0, 0.0, ALU.mult, ALU.add)
+
+        w1_codes = sb.tile([P, R], U32, name="w1_codes", align_bytes=64)
+        w1_plane = quantise(interleave(nc.scalar.copy, w1_raw, R, "w1_bf", "slot_b"), R, "w1", w1_codes[:])
+
+        wo_raw = sb.tile([P, PACK, R], F32, name="wo_raw", tag="slot_a", align_bytes=64)
+        nc.scalar.dma_start(wo_raw[:], wo.rearrange("(p j) r -> p j r", j=PACK))
+
+        dy_raw = sb.tile([P, PACK, M], F32, name="dy_raw", tag="slot_b", align_bytes=64)
+        nc.scalar.dma_start(dy_raw[:], dy.rearrange("(p j) m -> p j m", j=PACK))
+
+        tab_planes, tab_codes = [], []
+        for half in range(2):
+            listed = entries(idx, half * HALF, (half + 1) * HALF)
+            plane = sb.tile([P, HALF], U8, name="tab_plane%d" % half, align_bytes=64)
+            nc.vector.tensor_copy(plane[:], scales[:].indirect(listed))
+            codes = sb.tile([P, HALF], U32, name="tab_codes%d" % half, align_bytes=64)
+            nc.vector.tensor_copy(codes[:], words[:].bitcast(U32).indirect(listed))
+            tab_planes.append(plane)
+            tab_codes.append(codes)
+
+        pb_rows = sb.tile([P, M], F32, name="pb_rows", tag="slot_c", align_bytes=64)
+        nc.sync.dma_start(pb_rows[:], pb[0].partition_broadcast(P))
+
+        h1_sq = sb.tile([P, J], F32, name="h1_sq")
+
+        def forward(lo, hi, tag):
+            half, cols = lo // HALF, slice(lo % HALF, lo % HALF + hi - lo)
+            a = ps.tile([P, hi - lo], F32, name="a%d" % lo)
+            nc.tensor.matmul_mx(
+                out=a[:],
+                lhsT=w1_codes[:].bitcast(FP8X4),
+                lhsT_scale=w1_plane[:],
+                rhs=tab_codes[half][:, cols].bitcast(FP8X4),
+                rhs_scale=tab_planes[half][:, cols],
+                start=True,
+                stop=True,
+            )
+            h1 = sb.tile([P, hi - lo], F32, name="h1_%d" % lo, tag=tag, align_bytes=64)
+            nc.scalar.activation(h1[:], a[:], ACT.Tanh)
+            nc.vector.tensor_tensor(pg[:].indirect(entries(idx2, lo, hi)), h1[:], gain_rows[:, : hi - lo], ALU.mult)
+            return h1
+
+        h1_a = forward(0, 256, "h1_a")
+        wo_bf = interleave(nc.scalar.copy, wo_raw, R, "wo_bf", "tab_codes0")
+        wo_codes = sb.tile([P, R], U32, name="wo_codes", align_bytes=64)
+        wo_plane = quantise(wo_bf, R, "wo", wo_codes[:])
+        h1_b = forward(256, 384, "h1_b")
+        dy_bf = interleave(nc.scalar.copy, dy_raw, M, "dy_bf", "dy_bf")
+        dy_codes = sb.tile([P, M], U32, name="dy_codes", align_bytes=64)
+        dy_plane = quantise(dy_bf, M, "dy", dy_codes[:])
+        h1_c = forward(384, 512, "slot_b")
+
+        old_sb = sb.tile([P, J], F32, name="old_sb", tag="slot_d", align_bytes=64)
+        nc.sync.dma_start(old_sb[:], old)
+
+        s = sb.tile([P, M], F32, name="s")
+        nc.vector.tensor_tensor(s[:], pg[:].indirect(idx3[:]), pb_rows[:], ALU.add)
+
+        c0 = ps.tile([P, M], F32, name="c0")
+        nc.tensor.matmul_mx(
+            out=c0[:],
+            lhsT=wo_codes[:].bitcast(FP8X4),
+            lhsT_scale=wo_plane[:],
+            rhs=dy_codes[:].bitcast(FP8X4),
+            rhs_scale=dy_plane[:],
+            start=True,
+            stop=True,
+        )
+
+        t = sb.tile([P, M], F32, name="t")
+        z = sb.tile([P, M], F32, name="z")
+        x = sb.tile([P, M], F32, name="x")
+        y = sb.tile([P, M], F32, name="y")
+        for lo, hi in PICK_PIECES:
+            nc.scalar.activation(t[:, lo:hi], s[:, lo:hi], ACT.Tanh, scale=0.5)
+        nc.scalar.activation(z[:], t[:], ACT.Copy, scale=-0.25, bias=-0.25)
+        for lo, hi in PICK_PIECES:
+            nc.vector.scalar_tensor_tensor(x[:, lo:hi], t[:, lo:hi], 1.0, s[:, lo:hi], ALU.subtract, ALU.mult)
+        for lo, hi in PICK_PIECES:
+            nc.vector.scalar_tensor_tensor(y[:, lo:hi], x[:, lo:hi], 2.0, c0[:, lo:hi], ALU.subtract, ALU.mult)
+        for lo, hi in ((0, M),):
+            nc.vector.tensor_tensor(s1[:].indirect(idx3[:]), y[:, lo:hi], z[:, lo:hi], ALU.mult)
+
+        slope = sb.tile([P, J], F32, name="slope")
+        for h1, lo, hi in ((h1_a, 0, 256), (h1_b, 256, 384), (h1_c, 384, 512)):
+            nc.scalar.activation(h1_sq[:, lo:hi], h1[:], ACT.Square)
+        nc.scalar.activation(slope[:], h1_sq[:], ACT.Identity, scale=minus_gain[:], bias=gain_col[:])
+
+        da = sb.tile([P, J], F32, name="da")
+        result = sb.tile([P, J], F32, name="result")
+        for lo, hi in OUT_PIECES:
+            nc.vector.tensor_tensor(
+                da[:, lo:hi], s1[:].indirect(entries(idx2, lo, hi)), slope[:, lo:hi], ALU.mult
+            )
+        for lo, hi in OUT_PIECES:
+            nc.vector.tensor_tensor(result[:, lo:hi], da[:, lo:hi], old_sb[:, lo:hi], ALU.add)
+            (nc.sync if lo == 0 else nc.scalar).dma_start(out[:, lo:hi], result[:, lo:hi])

@@ -20,6 +20,7 @@ PACK = 4
 GROUP = 16
 HALF = J // 2
 SLOT_PIECES = ((0, 128), (128, 256), (256, 512))
+SCATTER_PIECES = ((0, 128), (128, 512))
 PICK_PIECES = ((0, 128), (128, 256))
 OUT_PIECES = ((0, 256), (256, 512))
 
@@ -32,6 +33,7 @@ def tile_attend_cwriteread_kernel(tc, tab_words, tab_scales, w1, gain, pb, wo, d
     nc = tc.nc
     with ExitStack() as ctx:
         sb = ctx.enter_context(tc.tile_pool(name="sb", bufs=1))
+        shared = ctx.enter_context(tc.tile_pool(name="shared", bufs=1))
         ps = ctx.enter_context(tc.psum_pool(name="ps", bufs=1))
 
         idx = sb.tile([P, J // GROUP], U16, name="idx")
@@ -39,28 +41,26 @@ def tile_attend_cwriteread_kernel(tc, tab_words, tab_scales, w1, gain, pb, wo, d
         idx3 = sb.tile([P, M // GROUP], U16, name="idx3")
         words = sb.tile([P, T], I32, name="words", tag="slot_d", align_bytes=64)
         scales = sb.tile([P, T], U8, name="scales", tag="slot_c", align_bytes=64)
-        w1_raw = sb.tile([P, PACK, R], F32, name="w1_raw", tag="slot_a", align_bytes=64)
-        gain_col = sb.tile([P, 1], F32, name="gain_col")
+        w1_raw = shared.tile([P, PACK, R], F32, name="w1_raw", offset=1088, align_bytes=64)
         pg = sb.tile([P, U], F32, name="pg")
         s1 = sb.tile([P, U], F32, name="s1")
 
         nc.vector.memset(scales[:].bitcast(I32), 0)
         nc.sync.dma_start(idx[:], offs)
-        nc.scalar.dma_start(w1_raw[:], w1.rearrange("(p j) r -> p j r", j=PACK))
-        nc.scalar.dma_start(words[:], tab_words[0].rearrange("p n t -> p (n t)").bitcast(I32))
+        nc.sync.dma_start(w1_raw[:], w1.rearrange("(p j) r -> p j r", j=PACK))
+        nc.sync.dma_start(idx2[:], offs2)
+        nc.sync.dma_start(idx3[:], offs3)
+        nc.sync.dma_start(words[:], tab_words[0].rearrange("p n t -> p (n t)").bitcast(I32))
         for q in range(4):
-            nc.sync.dma_start(
+            nc.scalar.dma_start(
                 scales[32 * q : 32 * q + 4, :].bitcast(I32),
                 tab_scales[0, 4 * q : 4 * q + 4, :].bitcast(I32),
             )
-        nc.gpsimd.dma_start(gain_col[:], gain)
-        nc.sync.dma_start(idx2[:], offs2)
-        nc.sync.dma_start(idx3[:], offs3)
         nc.vector.memset(pg[:], 0.0)
         nc.vector.memset(s1[:], 0.0)
 
-        def interleave(copy, raw, width, name, tag):
-            grouped = sb.tile([P, width, PACK], BF16, name=name, tag=tag, align_bytes=64)
+        def interleave(copy, raw, width, name, offset):
+            grouped = shared.tile([P, width, PACK], BF16, name=name, offset=offset, align_bytes=64)
             copy(grouped[:], raw[:].rearrange("p j w -> p w j"))
             return grouped
 
@@ -73,36 +73,38 @@ def tile_attend_cwriteread_kernel(tc, tab_words, tab_scales, w1, gain, pb, wo, d
             )
             return plane
 
-        gain_rows = sb.tile([P, HALF], F32, name="gain_rows")
-        nc.gpsimd.tensor_scalar(gain_rows[:], gain_col[:].to_broadcast([P, HALF]), 1.0, 0.0, ALU.mult, ALU.add)
+        w1_codes = sb.tile([P, R], U32, name="w1_codes", align_bytes=64)
+        w1_plane = quantise(interleave(nc.vector.tensor_copy, w1_raw, R, "w1_bf", 6400), R, "w1", w1_codes[:])
+
+        gain_col = shared.tile([P, 1], F32, name="gain_col", offset=2048, align_bytes=64)
+        nc.sync.dma_start(gain_col[:], gain)
+        wo_raw = shared.tile([P, PACK, R], F32, name="wo_raw", offset=0, align_bytes=64)
+        nc.sync.dma_start(wo_raw[:], wo.rearrange("(p j) r -> p j r", j=PACK))
+        dy_raw = shared.tile([P, PACK, M], F32, name="dy_raw", offset=2112, align_bytes=64)
+        nc.sync.dma_start(dy_raw[:], dy.rearrange("(p j) m -> p j m", j=PACK))
+
+        gain_rows = sb.tile([P, 384], F32, name="gain_rows")
+        nc.gpsimd.tensor_scalar(gain_rows[:], gain_col[:].to_broadcast([P, 384]), 1.0, 0.0, ALU.mult, ALU.add)
         minus_gain = sb.tile([P, 1], F32, name="minus_gain")
         nc.gpsimd.tensor_scalar(minus_gain[:], gain_col[:], -1.0, 0.0, ALU.mult, ALU.add)
 
-        w1_codes = sb.tile([P, R], U32, name="w1_codes", align_bytes=64)
-        w1_plane = quantise(interleave(nc.scalar.copy, w1_raw, R, "w1_bf", "slot_b"), R, "w1", w1_codes[:])
-
-        wo_raw = sb.tile([P, PACK, R], F32, name="wo_raw", tag="slot_a", align_bytes=64)
-        nc.scalar.dma_start(wo_raw[:], wo.rearrange("(p j) r -> p j r", j=PACK))
-
-        dy_raw = sb.tile([P, PACK, M], F32, name="dy_raw", tag="slot_b", align_bytes=64)
-        nc.scalar.dma_start(dy_raw[:], dy.rearrange("(p j) m -> p j m", j=PACK))
-
-        tab_planes, tab_codes = [], []
-        for half in range(2):
-            listed = entries(idx, half * HALF, (half + 1) * HALF)
-            plane = sb.tile([P, HALF], U8, name="tab_plane%d" % half, align_bytes=64)
-            nc.vector.tensor_copy(plane[:], scales[:].indirect(listed))
-            codes = sb.tile([P, HALF], U32, name="tab_codes%d" % half, align_bytes=64)
-            nc.vector.tensor_copy(codes[:], words[:].bitcast(U32).indirect(listed))
-            tab_planes.append(plane)
+        tab_plane = shared.tile([P, J], U8, name="tab_plane", offset=6400, align_bytes=64)
+        nc.vector.tensor_copy(tab_plane[:], scales[:].indirect(idx[:]))
+        tab_codes = []
+        for half, offset in enumerate((6912, 8448)):
+            codes = shared.tile([P, HALF], U32, name="tab_codes%d" % half, offset=offset, align_bytes=64)
+            nc.vector.tensor_copy(
+                codes[:], words[:].bitcast(U32).indirect(entries(idx, half * HALF, (half + 1) * HALF))
+            )
             tab_codes.append(codes)
 
         pb_rows = sb.tile([P, M], F32, name="pb_rows", tag="slot_c", align_bytes=64)
         nc.sync.dma_start(pb_rows[:], pb[0].partition_broadcast(P))
 
-        h1_sq = sb.tile([P, J], F32, name="h1_sq")
+        wo_bf = interleave(nc.scalar.copy, wo_raw, R, "wo_bf", 11008)
 
-        def forward(lo, hi, tag):
+        h1 = sb.tile([P, J], F32, name="h1")
+        for lo, hi in SLOT_PIECES:
             half, cols = lo // HALF, slice(lo % HALF, lo % HALF + hi - lo)
             a = ps.tile([P, hi - lo], F32, name="a%d" % lo)
             nc.tensor.matmul_mx(
@@ -110,29 +112,27 @@ def tile_attend_cwriteread_kernel(tc, tab_words, tab_scales, w1, gain, pb, wo, d
                 lhsT=w1_codes[:].bitcast(FP8X4),
                 lhsT_scale=w1_plane[:],
                 rhs=tab_codes[half][:, cols].bitcast(FP8X4),
-                rhs_scale=tab_planes[half][:, cols],
+                rhs_scale=tab_plane[:, lo:hi],
                 start=True,
                 stop=True,
             )
-            h1 = sb.tile([P, hi - lo], F32, name="h1_%d" % lo, tag=tag, align_bytes=64)
-            nc.scalar.activation(h1[:], a[:], ACT.Tanh)
-            nc.vector.tensor_tensor(pg[:].indirect(entries(idx2, lo, hi)), h1[:], gain_rows[:, : hi - lo], ALU.mult)
-            return h1
-
-        h1_a = forward(0, 256, "h1_a")
-        wo_bf = interleave(nc.scalar.copy, wo_raw, R, "wo_bf", "tab_codes0")
+            nc.scalar.activation(h1[:, lo:hi], a[:], ACT.Tanh)
         wo_codes = sb.tile([P, R], U32, name="wo_codes", align_bytes=64)
-        wo_plane = quantise(wo_bf, R, "wo", wo_codes[:])
-        h1_b = forward(256, 384, "h1_b")
-        dy_bf = interleave(nc.scalar.copy, dy_raw, M, "dy_bf", "dy_bf")
-        dy_codes = sb.tile([P, M], U32, name="dy_codes", align_bytes=64)
-        dy_plane = quantise(dy_bf, M, "dy", dy_codes[:])
-        h1_c = forward(384, 512, "slot_b")
+        for lo, hi in SCATTER_PIECES:
+            nc.vector.tensor_tensor(
+                pg[:].indirect(entries(idx2, lo, hi)), h1[:, lo:hi], gain_rows[:, : hi - lo], ALU.mult
+            )
+            if lo == 0:
+                wo_plane = quantise(wo_bf, R, "wo", wo_codes[:])
+
+        dy_bf = interleave(nc.scalar.copy, dy_raw, M, "dy_bf", 8960)
 
         old_sb = sb.tile([P, J], F32, name="old_sb", tag="slot_d", align_bytes=64)
         nc.sync.dma_start(old_sb[:], old)
 
-        s = sb.tile([P, M], F32, name="s")
+        dy_codes = sb.tile([P, M], U32, name="dy_codes", align_bytes=64)
+        dy_plane = quantise(dy_bf, M, "dy", dy_codes[:])
+        s = shared.tile([P, M], F32, name="s", offset=4096, align_bytes=64)
         nc.vector.tensor_tensor(s[:], pg[:].indirect(idx3[:]), pb_rows[:], ALU.add)
 
         c0 = ps.tile([P, M], F32, name="c0")
@@ -161,8 +161,8 @@ def tile_attend_cwriteread_kernel(tc, tab_words, tab_scales, w1, gain, pb, wo, d
             nc.vector.tensor_tensor(s1[:].indirect(idx3[:]), y[:, lo:hi], z[:, lo:hi], ALU.mult)
 
         slope = sb.tile([P, J], F32, name="slope")
-        for h1, lo, hi in ((h1_a, 0, 256), (h1_b, 256, 384), (h1_c, 384, 512)):
-            nc.scalar.activation(h1_sq[:, lo:hi], h1[:], ACT.Square)
+        h1_sq = sb.tile([P, J], F32, name="h1_sq")
+        nc.scalar.activation(h1_sq[:], h1[:], ACT.Square)
         nc.scalar.activation(slope[:], h1_sq[:], ACT.Identity, scale=minus_gain[:], bias=gain_col[:])
 
         da = sb.tile([P, J], F32, name="da")

@@ -1,6 +1,7 @@
 from contextlib import ExitStack
 
 import concourse.mybir as mybir
+from concourse.masks import make_identity
 
 K, R, F, T, J, U, M = 512, 128, 512, 2048, 512, 1024, 256
 FLOPS = 2 * K * R * J + 2 * F * R * M
@@ -18,11 +19,30 @@ ALU = mybir.AluOpType
 P = 128
 PACK = 4
 GROUP = 16
+QUADRANT = 32
+ALIGN = 64
 HALF = J // 2
-SLOT_PIECES = ((0, 128), (128, 256), (256, 512))
-SCATTER_PIECES = ((0, 128), (128, 512))
-PICK_PIECES = ((0, 128), (128, 256))
-OUT_PIECES = ((0, 256), (256, 512))
+PICK_HALF = M // 2
+LINE = 4
+
+WO_RAW = 0
+GAIN_COL = WO_RAW + 4 * PACK * R
+PB_COLS = GAIN_COL + ALIGN
+IDENTITY = PB_COLS + ALIGN
+DY_RAW = IDENTITY + 4 * P
+W1_RAW = GAIN_COL - 4 * P
+H1_SQ = DY_RAW
+S_PICK = H1_SQ + 4 * J
+W1_BF = DY_RAW + 4 * PACK * M
+PLANE_0 = W1_BF
+CODES_0 = PLANE_0 + HALF
+PB_ROWS = CODES_0 + 4 * HALF
+WO_CODES = PB_ROWS + 4 * M
+DY_BF = WO_CODES + 4 * R
+CODES_1 = WO_CODES - HALF
+ONES = DY_BF + 2 * PACK * M
+PLANE_1 = ONES
+H1 = PLANE_1 + HALF
 
 
 def entries(offsets, lo, hi):
@@ -36,141 +56,160 @@ def tile_attend_cwriteread_kernel(tc, tab_words, tab_scales, w1, gain, pb, wo, d
         shared = ctx.enter_context(tc.tile_pool(name="shared", bufs=1))
         ps = ctx.enter_context(tc.psum_pool(name="ps", bufs=1))
 
-        idx = sb.tile([P, J // GROUP], U16, name="idx")
-        idx2 = sb.tile([P, J // GROUP], U16, name="idx2")
-        idx3 = sb.tile([P, M // GROUP], U16, name="idx3")
-        words = sb.tile([P, T], I32, name="words", tag="slot_d", align_bytes=64)
-        scales = sb.tile([P, T], U8, name="scales", tag="slot_c", align_bytes=64)
-        w1_raw = shared.tile([P, PACK, R], F32, name="w1_raw", offset=1088, align_bytes=64)
-        pg = sb.tile([P, U], F32, name="pg")
-        s1 = sb.tile([P, U], F32, name="s1")
+        def placed(name, shape, dtype, offset):
+            return shared.tile(shape, dtype, name=name, offset=offset, align_bytes=ALIGN)
 
-        nc.vector.memset(scales[:].bitcast(I32), 0)
-        nc.sync.dma_start(idx[:], offs)
-        nc.sync.dma_start(w1_raw[:], w1.rearrange("(p j) r -> p j r", j=PACK))
-        nc.sync.dma_start(idx2[:], offs2)
-        nc.sync.dma_start(idx3[:], offs3)
-        nc.sync.dma_start(words[:], tab_words[0].rearrange("p n t -> p (n t)").bitcast(I32))
-        for q in range(4):
-            nc.scalar.dma_start(
-                scales[32 * q : 32 * q + 4, :].bitcast(I32),
-                tab_scales[0, 4 * q : 4 * q + 4, :].bitcast(I32),
+        def load_rows(raw, matrix):
+            nc.sync.dma_start(raw[:], matrix.rearrange("(p j) w -> p j w", j=PACK))
+
+        def interleave(copy, grouped, raw):
+            copy(
+                grouped.rearrange("p (c i) j -> p c j i", i=LINE),
+                raw.rearrange("p j (c i) -> p c j i", i=LINE),
             )
-        nc.vector.memset(pg[:], 0.0)
-        nc.vector.memset(s1[:], 0.0)
 
-        def interleave(copy, raw, width, name, offset):
-            grouped = shared.tile([P, width, PACK], BF16, name=name, offset=offset, align_bytes=64)
-            copy(grouped[:], raw[:].rearrange("p j w -> p w j"))
-            return grouped
-
-        def quantise(grouped, width, name, codes):
-            plane = sb.tile([P, width], U8, name=name + "_plane", align_bytes=64)
+        def quantise(codes, grouped, name):
+            plane = sb.tile([P, codes.shape[1]], U8, name=name, align_bytes=ALIGN)
             nc.vector.quantize_mx(
-                out=codes.bitcast(FP8X4),
-                scales=plane[:],
-                in_=grouped[:].rearrange("p w j -> p (w j)"),
+                out=codes[:].bitcast(FP8X4), scales=plane[:], in_=grouped[:].rearrange("p w j -> p (w j)")
             )
             return plane
 
-        w1_codes = sb.tile([P, R], U32, name="w1_codes", align_bytes=64)
-        w1_plane = quantise(interleave(nc.vector.tensor_copy, w1_raw, R, "w1_bf", 6400), R, "w1", w1_codes[:])
-
-        gain_col = shared.tile([P, 1], F32, name="gain_col", offset=2048, align_bytes=64)
-        nc.sync.dma_start(gain_col[:], gain)
-        wo_raw = shared.tile([P, PACK, R], F32, name="wo_raw", offset=0, align_bytes=64)
-        nc.sync.dma_start(wo_raw[:], wo.rearrange("(p j) r -> p j r", j=PACK))
-        dy_raw = shared.tile([P, PACK, M], F32, name="dy_raw", offset=2112, align_bytes=64)
-        nc.sync.dma_start(dy_raw[:], dy.rearrange("(p j) m -> p j m", j=PACK))
-
-        gain_rows = sb.tile([P, 384], F32, name="gain_rows")
-        nc.gpsimd.tensor_scalar(gain_rows[:], gain_col[:].to_broadcast([P, 384]), 1.0, 0.0, ALU.mult, ALU.add)
-        minus_gain = sb.tile([P, 1], F32, name="minus_gain")
-        nc.gpsimd.tensor_scalar(minus_gain[:], gain_col[:], -1.0, 0.0, ALU.mult, ALU.add)
-
-        tab_plane = shared.tile([P, J], U8, name="tab_plane", offset=6400, align_bytes=64)
-        nc.vector.tensor_copy(tab_plane[:], scales[:].indirect(idx[:]))
-        tab_codes = []
-        for half, offset in enumerate((6912, 8448)):
-            codes = shared.tile([P, HALF], U32, name="tab_codes%d" % half, offset=offset, align_bytes=64)
-            nc.vector.tensor_copy(
-                codes[:], words[:].bitcast(U32).indirect(entries(idx, half * HALF, (half + 1) * HALF))
-            )
-            tab_codes.append(codes)
-
-        pb_rows = sb.tile([P, M], F32, name="pb_rows", tag="slot_c", align_bytes=64)
-        nc.sync.dma_start(pb_rows[:], pb[0].partition_broadcast(P))
-
-        wo_bf = interleave(nc.scalar.copy, wo_raw, R, "wo_bf", 11008)
-
-        h1 = sb.tile([P, J], F32, name="h1")
-        for lo, hi in SLOT_PIECES:
-            half, cols = lo // HALF, slice(lo % HALF, lo % HALF + hi - lo)
-            a = ps.tile([P, hi - lo], F32, name="a%d" % lo)
+        def product(acc, lhs_codes, lhs_plane, rhs_codes, rhs_plane):
             nc.tensor.matmul_mx(
-                out=a[:],
-                lhsT=w1_codes[:].bitcast(FP8X4),
-                lhsT_scale=w1_plane[:],
-                rhs=tab_codes[half][:, cols].bitcast(FP8X4),
-                rhs_scale=tab_plane[:, lo:hi],
+                out=acc[:],
+                lhsT=lhs_codes[:].bitcast(FP8X4),
+                lhsT_scale=lhs_plane[:],
+                rhs=rhs_codes[:].bitcast(FP8X4),
+                rhs_scale=rhs_plane[:],
                 start=True,
                 stop=True,
             )
-            nc.scalar.activation(h1[:, lo:hi], a[:], ACT.Tanh)
-        wo_codes = sb.tile([P, R], U32, name="wo_codes", align_bytes=64)
-        for lo, hi in SCATTER_PIECES:
-            nc.vector.tensor_tensor(
-                pg[:].indirect(entries(idx2, lo, hi)), h1[:, lo:hi], gain_rows[:, : hi - lo], ALU.mult
+
+        idx = sb.tile([P, J // GROUP], U16, name="idx")
+        idx2 = sb.tile([P, J // GROUP], U16, name="idx2")
+        idx3 = sb.tile([P, M // GROUP], U16, name="idx3")
+        words = sb.tile([P, T], I32, name="words", tag="words_then_old")
+        scales = sb.tile([P, T], U8, name="scales", tag="scales_then_wo_bf", align_bytes=ALIGN)
+        w1_raw = placed("w1_raw", [P, PACK, R], F32, W1_RAW)
+
+        nc.vector.memset(scales[:].bitcast(I32), 0)
+        nc.sync.dma_start(idx[:], offs)
+        load_rows(w1_raw, w1)
+        nc.sync.dma_start(idx2[:], offs2)
+        nc.sync.dma_start(idx3[:], offs3)
+        nc.sync.dma_start(words[:], tab_words[0].rearrange("p n t -> p (n t)").bitcast(I32))
+        for q in range(P // QUADRANT):
+            nc.scalar.dma_start(
+                scales[QUADRANT * q : QUADRANT * q + PACK, :].bitcast(I32),
+                tab_scales[0, PACK * q : PACK * (q + 1), :].bitcast(I32),
             )
-            if lo == 0:
-                wo_plane = quantise(wo_bf, R, "wo", wo_codes[:])
+        ones = placed("ones", [P, HALF], F32, ONES)
+        pg = sb.tile([P, U], F32, name="pg")
+        s1 = sb.tile([P, U], F32, name="s1")
+        nc.vector.memset(ones[:], 1.0)
+        nc.vector.memset(pg[:], 0.0)
+        nc.vector.memset(s1[:], 0.0)
 
-        dy_bf = interleave(nc.scalar.copy, dy_raw, M, "dy_bf", 8960)
+        w1_bf = placed("w1_bf", [P, R, PACK], BF16, W1_BF)
+        interleave(nc.vector.tensor_copy, w1_bf[:], w1_raw[:])
+        w1_codes = sb.tile([P, R], U32, name="w1_codes", align_bytes=ALIGN)
+        w1_plane = quantise(w1_codes, w1_bf, "w1_plane")
 
-        old_sb = sb.tile([P, J], F32, name="old_sb", tag="slot_d", align_bytes=64)
+        gain_col = placed("gain_col", [P, 1], F32, GAIN_COL)
+        wo_raw = placed("wo_raw", [P, PACK, R], F32, WO_RAW)
+        dy_raw = placed("dy_raw", [P, PACK, M], F32, DY_RAW)
+        pb_cols = placed("pb_cols", [P, M // P], F32, PB_COLS)
+        nc.sync.dma_start(gain_col[:], gain)
+        load_rows(wo_raw, wo)
+        load_rows(dy_raw, dy)
+        nc.sync.dma_start(pb_cols[:], pb.rearrange("o (p c) -> (o p) c", p=P))
+        identity = placed("identity", [P, P], F32, IDENTITY)
+        make_identity(nc, identity[:])
+
+        minus_gain = sb.tile([P, 1], F32, name="minus_gain")
+        nc.scalar.activation(minus_gain[:], gain_col[:], ACT.Copy, scale=-1.0)
+        gain_rows = sb.tile([P, HALF], F32, name="gain_rows")
+        nc.scalar.activation(gain_rows[:], ones[:], ACT.Copy, scale=gain_col[:])
+
+        h1 = placed("h1", [P, J], F32, H1)
+        codes = [placed("codes_%d" % h, [P, HALF], U32, at) for h, at in enumerate((CODES_0, CODES_1))]
+        planes = [placed("plane_%d" % h, [P, HALF], U8, at) for h, at in enumerate((PLANE_0, PLANE_1))]
+
+        def gather_scales(h):
+            nc.vector.tensor_copy(planes[h][:], scales[:].indirect(entries(idx, h * HALF, (h + 1) * HALF)))
+
+        def gather_words(h):
+            listed = entries(idx, h * HALF, (h + 1) * HALF)
+            nc.vector.tensor_copy(codes[h][:], words[:].bitcast(U32).indirect(listed))
+
+        def first_layer(h):
+            a = ps.tile([P, HALF], F32, name="a_%d" % h)
+            product(a, w1_codes, w1_plane, codes[h], planes[h])
+            nc.scalar.activation(h1[:, h * HALF : (h + 1) * HALF], a[:], ACT.Tanh)
+
+        def scatter_h2(h):
+            lo, hi = h * HALF, (h + 1) * HALF
+            nc.vector.tensor_tensor(pg[:].indirect(entries(idx2, lo, hi)), h1[:, lo:hi], gain_rows[:], ALU.mult)
+
+        gather_scales(0)
+        gather_words(0)
+        gather_words(1)
+        first_layer(0)
+        gather_scales(1)
+        wo_bf = sb.tile([P, R, PACK], BF16, name="wo_bf", tag="scales_then_wo_bf", align_bytes=ALIGN)
+        interleave(nc.scalar.copy, wo_bf[:], wo_raw[:])
+        first_layer(1)
+        scatter_h2(0)
+        wo_codes = placed("wo_codes", [P, R], U32, WO_CODES)
+        wo_plane = quantise(wo_codes, wo_bf, "wo_plane")
+        scatter_h2(1)
+
+        old_sb = sb.tile([P, J], F32, name="old_sb", tag="words_then_old")
         nc.sync.dma_start(old_sb[:], old)
 
-        dy_codes = sb.tile([P, M], U32, name="dy_codes", align_bytes=64)
-        dy_plane = quantise(dy_bf, M, "dy", dy_codes[:])
-        s = shared.tile([P, M], F32, name="s", offset=4096, align_bytes=64)
-        nc.vector.tensor_tensor(s[:], pg[:].indirect(idx3[:]), pb_rows[:], ALU.add)
+        dy_bf = placed("dy_bf", [P, M, PACK], BF16, DY_BF)
+        pick_halves = [slice(lo, lo + PICK_HALF) for lo in range(0, M, PICK_HALF)]
+        for cols in pick_halves:
+            interleave(nc.scalar.copy, dy_bf[:, cols, :], dy_raw[:, :, cols])
+        dy_codes = sb.tile([P, M], U32, name="dy_codes", align_bytes=ALIGN)
+        dy_plane = quantise(dy_codes, dy_bf, "dy_plane")
+
+        pb_turned = ps.tile([P, M // P, P], F32, name="pb_turned", tag="a_0")
+        for c in range(M // P):
+            nc.tensor.transpose(pb_turned[:, c, :], pb_cols[:, c : c + 1].to_broadcast([P, P]), identity[:])
+        pb_rows = placed("pb_rows", [P, M], F32, PB_ROWS)
+        nc.scalar.copy(pb_rows[:].rearrange("p (n c) -> p n c", c=M // P), pb_turned[:].rearrange("p c n -> p n c"))
 
         c0 = ps.tile([P, M], F32, name="c0")
-        nc.tensor.matmul_mx(
-            out=c0[:],
-            lhsT=wo_codes[:].bitcast(FP8X4),
-            lhsT_scale=wo_plane[:],
-            rhs=dy_codes[:].bitcast(FP8X4),
-            rhs_scale=dy_plane[:],
-            start=True,
-            stop=True,
-        )
+        product(c0, wo_codes, wo_plane, dy_codes, dy_plane)
 
+        s = placed("s", [P, M], F32, S_PICK)
+        nc.vector.tensor_tensor(s[:], pg[:].indirect(idx3[:]), pb_rows[:], ALU.add)
         t = sb.tile([P, M], F32, name="t")
-        z = sb.tile([P, M], F32, name="z")
-        x = sb.tile([P, M], F32, name="x")
-        y = sb.tile([P, M], F32, name="y")
-        for lo, hi in PICK_PIECES:
-            nc.scalar.activation(t[:, lo:hi], s[:, lo:hi], ACT.Tanh, scale=0.5)
-        nc.scalar.activation(z[:], t[:], ACT.Copy, scale=-0.25, bias=-0.25)
-        for lo, hi in PICK_PIECES:
-            nc.vector.scalar_tensor_tensor(x[:, lo:hi], t[:, lo:hi], 1.0, s[:, lo:hi], ALU.subtract, ALU.mult)
-        for lo, hi in PICK_PIECES:
-            nc.vector.scalar_tensor_tensor(y[:, lo:hi], x[:, lo:hi], 2.0, c0[:, lo:hi], ALU.subtract, ALU.mult)
-        for lo, hi in ((0, M),):
-            nc.vector.tensor_tensor(s1[:].indirect(idx3[:]), y[:, lo:hi], z[:, lo:hi], ALU.mult)
+        inner = sb.tile([P, M], F32, name="inner")
+        left = sb.tile([P, M], F32, name="left")
+        right = sb.tile([P, M], F32, name="right")
+        for cols in pick_halves:
+            nc.scalar.activation(t[:, cols], s[:, cols], ACT.Tanh, scale=0.5)
+        nc.scalar.activation(right[:], t[:], ACT.Copy, scale=-0.25, bias=-0.25)
+        for cols in pick_halves:
+            nc.vector.scalar_tensor_tensor(inner[:, cols], t[:, cols], 1.0, s[:, cols], ALU.subtract, ALU.mult)
+        for cols in pick_halves:
+            nc.vector.scalar_tensor_tensor(left[:, cols], inner[:, cols], 2.0, c0[:, cols], ALU.subtract, ALU.mult)
+        nc.vector.tensor_tensor(s1[:].indirect(idx3[:]), left[:], right[:], ALU.mult)
 
+        h1_sq = placed("h1_sq", [P, J], F32, H1_SQ)
         slope = sb.tile([P, J], F32, name="slope")
-        h1_sq = sb.tile([P, J], F32, name="h1_sq")
         nc.scalar.activation(h1_sq[:], h1[:], ACT.Square)
         nc.scalar.activation(slope[:], h1_sq[:], ACT.Identity, scale=minus_gain[:], bias=gain_col[:])
 
         da = sb.tile([P, J], F32, name="da")
         result = sb.tile([P, J], F32, name="result")
-        for lo, hi in OUT_PIECES:
-            nc.vector.tensor_tensor(
-                da[:, lo:hi], s1[:].indirect(entries(idx2, lo, hi)), slope[:, lo:hi], ALU.mult
-            )
-        for lo, hi in OUT_PIECES:
-            nc.vector.tensor_tensor(result[:, lo:hi], da[:, lo:hi], old_sb[:, lo:hi], ALU.add)
-            (nc.sync if lo == 0 else nc.scalar).dma_start(out[:, lo:hi], result[:, lo:hi])
+        for lo in range(0, J, HALF):
+            listed = entries(idx2, lo, lo + HALF)
+            nc.vector.tensor_tensor(da[:, lo : lo + HALF], s1[:].indirect(listed), slope[:, lo : lo + HALF], ALU.mult)
+        for lo, queue in ((0, nc.sync), (HALF, nc.scalar)):
+            cols = slice(lo, lo + HALF)
+            nc.vector.tensor_tensor(result[:, cols], da[:, cols], old_sb[:, cols], ALU.add)
+            queue.dma_start(out[:, cols], result[:, cols])

@@ -36,13 +36,13 @@ S_PICK = H1_SQ + 4 * J
 W1_BF = DY_RAW + 4 * PACK * M
 PLANE_0 = W1_BF
 CODES_0 = PLANE_0 + HALF
-PB_ROWS = CODES_0 + 4 * HALF
+H1 = CODES_0 + 4 * HALF
+PLANE_1 = H1 + 4 * J
+PB_ROWS = PLANE_1 + HALF
 WO_CODES = PB_ROWS + 4 * M
 DY_BF = WO_CODES + 4 * R
-CODES_1 = WO_CODES - HALF
-ONES = DY_BF + 2 * PACK * M
-PLANE_1 = ONES
-H1 = PLANE_1 + HALF
+CODES_1 = DY_BF + ALIGN - 4 * HALF
+ONES = PLANE_1 - ALIGN
 
 
 def entries(offsets, lo, hi):
@@ -93,6 +93,12 @@ def tile_attend_cwriteread_kernel(tc, tab_words, tab_scales, w1, gain, pb, wo, d
         scales = sb.tile([P, T], U8, name="scales", tag="scales_then_wo_bf", align_bytes=ALIGN)
         w1_raw = placed("w1_raw", [P, PACK, R], F32, W1_RAW)
 
+        ones = placed("ones", [P, HALF], F32, ONES)
+        pg = sb.tile([P, U], F32, name="pg")
+        s1 = sb.tile([P, U], F32, name="s1")
+        nc.vector.memset(ones[:], 1.0)
+        nc.vector.memset(pg[:], 0.0)
+        nc.vector.memset(s1[:], 0.0)
         nc.vector.memset(scales[:].bitcast(I32), 0)
         nc.sync.dma_start(idx[:], offs)
         load_rows(w1_raw, w1)
@@ -100,16 +106,10 @@ def tile_attend_cwriteread_kernel(tc, tab_words, tab_scales, w1, gain, pb, wo, d
         nc.sync.dma_start(idx3[:], offs3)
         nc.sync.dma_start(words[:], tab_words[0].rearrange("p n t -> p (n t)").bitcast(I32))
         for q in range(P // QUADRANT):
-            nc.scalar.dma_start(
+            nc.sync.dma_start(
                 scales[QUADRANT * q : QUADRANT * q + PACK, :].bitcast(I32),
                 tab_scales[0, PACK * q : PACK * (q + 1), :].bitcast(I32),
             )
-        ones = placed("ones", [P, HALF], F32, ONES)
-        pg = sb.tile([P, U], F32, name="pg")
-        s1 = sb.tile([P, U], F32, name="s1")
-        nc.vector.memset(ones[:], 1.0)
-        nc.vector.memset(pg[:], 0.0)
-        nc.vector.memset(s1[:], 0.0)
 
         w1_bf = placed("w1_bf", [P, R, PACK], BF16, W1_BF)
         interleave(nc.vector.tensor_copy, w1_bf[:], w1_raw[:])
@@ -152,8 +152,8 @@ def tile_attend_cwriteread_kernel(tc, tab_words, tab_scales, w1, gain, pb, wo, d
             lo, hi = h * HALF, (h + 1) * HALF
             nc.vector.tensor_tensor(pg[:].indirect(entries(idx2, lo, hi)), h1[:, lo:hi], gain_rows[:], ALU.mult)
 
-        gather_scales(0)
         gather_words(0)
+        gather_scales(0)
         gather_words(1)
         first_layer(0)
         gather_scales(1)

from contextlib import ExitStack

import concourse.mybir as mybir
from concourse.masks import make_identity

K, R, F, T, J, U, M = 512, 128, 512, 2048, 512, 1024, 256
FLOPS = 2 * K * R * J + 2 * F * R * M

F32 = mybir.dt.float32
BF16 = mybir.dt.bfloat16
I32 = mybir.dt.int32
U32 = mybir.dt.uint32
U16 = mybir.dt.uint16
U8 = mybir.dt.uint8
FP8X4 = mybir.dt.float8_e4m3fn_x4
ACT = mybir.ActivationFunctionType
ALU = mybir.AluOpType

P = 128
PACK = 4
GROUP = 16
QUADRANT = 32
ALIGN = 64
HALF = J // 2
PICK_HALF = M // 2
LINE = 4

WO_RAW = 0
GAIN_COL = WO_RAW + 4 * PACK * R
PB_COLS = GAIN_COL + ALIGN
IDENTITY = PB_COLS + ALIGN
DY_RAW = IDENTITY + 4 * P
W1_RAW = GAIN_COL - 4 * P
H1_SQ = DY_RAW
S_PICK = H1_SQ + 4 * J
W1_BF = DY_RAW + 4 * PACK * M
PLANE_0 = W1_BF
CODES_0 = PLANE_0 + HALF
H1 = CODES_0 + 4 * HALF
PLANE_1 = H1 + 4 * J
PB_ROWS = PLANE_1 + HALF
WO_CODES = PB_ROWS + 4 * M
DY_BF = WO_CODES + 4 * R
CODES_1 = DY_BF + ALIGN - 4 * HALF
ONES = PLANE_1 - ALIGN


def entries(offsets, lo, hi):
    return offsets[:, lo // GROUP : hi // GROUP]


def tile_attend_cwriteread_kernel(tc, tab_words, tab_scales, w1, gain, pb, wo, dy, old, offs, offs2, offs3, out):
    nc = tc.nc
    with ExitStack() as ctx:
        sb = ctx.enter_context(tc.tile_pool(name="sb", bufs=1))
        shared = ctx.enter_context(tc.tile_pool(name="shared", bufs=1))
        ps = ctx.enter_context(tc.psum_pool(name="ps", bufs=1))

        def placed(name, shape, dtype, offset):
            return shared.tile(shape, dtype, name=name, offset=offset, align_bytes=ALIGN)

        def load_rows(raw, matrix):
            nc.sync.dma_start(raw[:], matrix.rearrange("(p j) w -> p j w", j=PACK))

        def interleave(copy, grouped, raw):
            copy(
                grouped.rearrange("p (c i) j -> p c j i", i=LINE),
                raw.rearrange("p j (c i) -> p c j i", i=LINE),
            )

        def quantise(codes, grouped, name):
            plane = sb.tile([P, codes.shape[1]], U8, name=name, align_bytes=ALIGN)
            nc.vector.quantize_mx(
                out=codes[:].bitcast(FP8X4), scales=plane[:], in_=grouped[:].rearrange("p w j -> p (w j)")
            )
            return plane

        def product(acc, lhs_codes, lhs_plane, rhs_codes, rhs_plane):
            nc.tensor.matmul_mx(
                out=acc[:],
                lhsT=lhs_codes[:].bitcast(FP8X4),
                lhsT_scale=lhs_plane[:],
                rhs=rhs_codes[:].bitcast(FP8X4),
                rhs_scale=rhs_plane[:],
                start=True,
                stop=True,
            )

        idx = sb.tile([P, J // GROUP], U16, name="idx")
        idx2 = sb.tile([P, J // GROUP], U16, name="idx2")
        idx3 = sb.tile([P, M // GROUP], U16, name="idx3")
        words = sb.tile([P, T], I32, name="words", tag="words_then_old")
        scales = sb.tile([P, T], U8, name="scales", tag="scales_then_wo_bf", align_bytes=ALIGN)
        w1_raw = placed("w1_raw", [P, PACK, R], F32, W1_RAW)

        ones = placed("ones", [P, HALF], F32, ONES)
        pg = sb.tile([P, U], F32, name="pg")
        s1 = sb.tile([P, U], F32, name="s1")
        nc.vector.memset(ones[:], 1.0)
        nc.vector.memset(pg[:], 0.0)
        nc.vector.memset(s1[:], 0.0)
        nc.vector.memset(scales[:].bitcast(I32), 0)
        nc.sync.dma_start(idx[:], offs)
        load_rows(w1_raw, w1)
        nc.sync.dma_start(idx2[:], offs2)
        nc.sync.dma_start(idx3[:], offs3)
        nc.sync.dma_start(words[:], tab_words[0].rearrange("p n t -> p (n t)").bitcast(I32))
        for q in range(P // QUADRANT):
            nc.sync.dma_start(
                scales[QUADRANT * q : QUADRANT * q + PACK, :].bitcast(I32),
                tab_scales[0, PACK * q : PACK * (q + 1), :].bitcast(I32),
            )

        w1_bf = placed("w1_bf", [P, R, PACK], BF16, W1_BF)
        interleave(nc.vector.tensor_copy, w1_bf[:], w1_raw[:])
        w1_codes = sb.tile([P, R], U32, name="w1_codes", align_bytes=ALIGN)
        w1_plane = quantise(w1_codes, w1_bf, "w1_plane")

        gain_col = placed("gain_col", [P, 1], F32, GAIN_COL)
        wo_raw = placed("wo_raw", [P, PACK, R], F32, WO_RAW)
        dy_raw = placed("dy_raw", [P, PACK, M], F32, DY_RAW)
        pb_cols = placed("pb_cols", [P, M // P], F32, PB_COLS)
        nc.sync.dma_start(gain_col[:], gain)
        load_rows(wo_raw, wo)
        load_rows(dy_raw, dy)
        nc.sync.dma_start(pb_cols[:], pb.rearrange("o (p c) -> (o p) c", p=P))
        identity = placed("identity", [P, P], F32, IDENTITY)
        make_identity(nc, identity[:])

        minus_gain = sb.tile([P, 1], F32, name="minus_gain")
        nc.scalar.activation(minus_gain[:], gain_col[:], ACT.Copy, scale=-1.0)
        gain_rows = sb.tile([P, HALF], F32, name="gain_rows")
        nc.scalar.activation(gain_rows[:], ones[:], ACT.Copy, scale=gain_col[:])

        h1 = placed("h1", [P, J], F32, H1)
        codes = [placed("codes_%d" % h, [P, HALF], U32, at) for h, at in enumerate((CODES_0, CODES_1))]
        planes = [placed("plane_%d" % h, [P, HALF], U8, at) for h, at in enumerate((PLANE_0, PLANE_1))]

        def gather_scales(h):
            nc.vector.tensor_copy(planes[h][:], scales[:].indirect(entries(idx, h * HALF, (h + 1) * HALF)))

        def gather_words(h):
            listed = entries(idx, h * HALF, (h + 1) * HALF)
            nc.vector.tensor_copy(codes[h][:], words[:].bitcast(U32).indirect(listed))

        def first_layer(h):
            a = ps.tile([P, HALF], F32, name="a_%d" % h)
            product(a, w1_codes, w1_plane, codes[h], planes[h])
            nc.scalar.activation(h1[:, h * HALF : (h + 1) * HALF], a[:], ACT.Tanh)

        def scatter_h2(h):
            lo, hi = h * HALF, (h + 1) * HALF
            nc.vector.tensor_tensor(pg[:].indirect(entries(idx2, lo, hi)), h1[:, lo:hi], gain_rows[:], ALU.mult)

        gather_words(0)
        gather_scales(0)
        gather_words(1)
        first_layer(0)
        gather_scales(1)
        wo_bf = sb.tile([P, R, PACK], BF16, name="wo_bf", tag="scales_then_wo_bf", align_bytes=ALIGN)
        interleave(nc.scalar.copy, wo_bf[:], wo_raw[:])
        first_layer(1)
        scatter_h2(0)
        wo_codes = placed("wo_codes", [P, R], U32, WO_CODES)
        wo_plane = quantise(wo_codes, wo_bf, "wo_plane")
        scatter_h2(1)

        old_sb = sb.tile([P, J], F32, name="old_sb", tag="words_then_old")
        nc.sync.dma_start(old_sb[:], old)

        dy_bf = placed("dy_bf", [P, M, PACK], BF16, DY_BF)
        pick_halves = [slice(lo, lo + PICK_HALF) for lo in range(0, M, PICK_HALF)]
        for cols in pick_halves:
            interleave(nc.scalar.copy, dy_bf[:, cols, :], dy_raw[:, :, cols])
        dy_codes = sb.tile([P, M], U32, name="dy_codes", align_bytes=ALIGN)
        dy_plane = quantise(dy_codes, dy_bf, "dy_plane")

        pb_turned = ps.tile([P, M // P, P], F32, name="pb_turned", tag="a_0")
        for c in range(M // P):
            nc.tensor.transpose(pb_turned[:, c, :], pb_cols[:, c : c + 1].to_broadcast([P, P]), identity[:])
        pb_rows = placed("pb_rows", [P, M], F32, PB_ROWS)
        nc.scalar.copy(pb_rows[:].rearrange("p (n c) -> p n c", c=M // P), pb_turned[:].rearrange("p c n -> p n c"))

        c0 = ps.tile([P, M], F32, name="c0")
        product(c0, wo_codes, wo_plane, dy_codes, dy_plane)

        s = placed("s", [P, M], F32, S_PICK)
        nc.vector.tensor_tensor(s[:], pg[:].indirect(idx3[:]), pb_rows[:], ALU.add)
        t = sb.tile([P, M], F32, name="t")
        inner = sb.tile([P, M], F32, name="inner")
        left = sb.tile([P, M], F32, name="left")
        right = sb.tile([P, M], F32, name="right")
        for cols in pick_halves:
            nc.scalar.activation(t[:, cols], s[:, cols], ACT.Tanh, scale=0.5)
        nc.scalar.activation(right[:], t[:], ACT.Copy, scale=-0.25, bias=-0.25)
        for cols in pick_halves:
            nc.vector.scalar_tensor_tensor(inner[:, cols], t[:, cols], 1.0, s[:, cols], ALU.subtract, ALU.mult)
        for cols in pick_halves:
            nc.vector.scalar_tensor_tensor(left[:, cols], inner[:, cols], 2.0, c0[:, cols], ALU.subtract, ALU.mult)
        nc.vector.tensor_tensor(s1[:].indirect(idx3[:]), left[:], right[:], ALU.mult)

        h1_sq = placed("h1_sq", [P, J], F32, H1_SQ)
        slope = sb.tile([P, J], F32, name="slope")
        nc.scalar.activation(h1_sq[:], h1[:], ACT.Square)
        nc.scalar.activation(slope[:], h1_sq[:], ACT.Identity, scale=minus_gain[:], bias=gain_col[:])

        da = sb.tile([P, J], F32, name="da")
        result = sb.tile([P, J], F32, name="result")
        for lo in range(0, J, HALF):
            listed = entries(idx2, lo, lo + HALF)
            nc.vector.tensor_tensor(da[:, lo : lo + HALF], s1[:].indirect(listed), slope[:, lo : lo + HALF], ALU.mult)
        for lo, queue in ((0, nc.sync), (HALF, nc.scalar)):
            cols = slice(lo, lo + HALF)
            nc.vector.tensor_tensor(result[:, cols], da[:, cols], old_sb[:, cols], ALU.add)
            queue.dma_start(out[:, cols], result[:, cols])
